import numpy as np
import ml_dtypes


def mxq(x, axis, fmt="e4m3"):
    dtype, down = {"e4m3": (ml_dtypes.float8_e4m3fn, 7), "e5m2": (ml_dtypes.float8_e5m2, 14)}[fmt]
    v = np.moveaxis(np.asarray(x, np.float32).astype(ml_dtypes.bfloat16).astype(np.float64), axis, -1)
    blocks = v.reshape(v.shape[:-1] + (-1, 32))
    amax = np.abs(blocks).max(-1, keepdims=True)
    byte = np.maximum(np.where(amax > 0, np.frexp(amax)[1] - 1 + 127, 0) - down, 1)
    scale = np.exp2(byte - 127.0)
    codes = (blocks / scale).astype(np.float32).astype(dtype).astype(np.float64)
    return np.moveaxis((codes * scale).reshape(v.shape), -1, axis)


WIDE = False


def mx_kscale(k):
    if not WIDE:
        return np.ones(k)
    levels = np.array([30, -30])
    if k % 512:
        return np.exp2(np.random.permutation(np.resize(levels, k // 32))).repeat(32)
    a = np.empty((k // 512, 16))
    for p in range(k // 512):
        a[p, :8] = np.random.permutation(np.resize(levels, 8))
        for g in range(8):
            far = levels[np.abs(levels - a[p, g]) >= 10]
            a[p, g + 8] = far[np.random.randint(len(far))]
    return np.exp2(a.ravel()).repeat(32)


def f64(x):
    return np.asarray(x).astype(np.float64)


def striped(idx):
    return np.tile(np.asarray(idx).reshape(-1, 16).T, (8, 1)).astype(np.uint16)


def unstriped(offs):
    return offs[:16].T.reshape(-1).astype(np.int64)


E2M1 = np.array([0.0, 0.5, 1.0, 1.5, 2.0, 3.0, 4.0, 6.0, -0.0, -0.5, -1.0, -1.5, -2.0, -3.0, -4.0, -6.0])


def pack_weight(w, fmt):
    k, n = w.shape
    w = f64(np.asarray(w, np.float32).astype(ml_dtypes.bfloat16)).reshape(k // 32, 32, n)
    amax = np.abs(w).max(1)
    if fmt == "e4m3":
        byte = np.frexp(amax)[1] - 1 + 127 - 7
    else:
        mant, ex = np.frexp(amax / 6.0)
        byte = np.where(mant > 0.5, ex, ex - 1) + 127
    byte = np.clip(np.where(amax > 0, byte, 1), 1, 254)
    scaled = (w * np.exp2(127.0 - byte)[:, None, :]).reshape(k, n).astype(np.float32)
    by_word = np.ascontiguousarray(scaled.reshape(k // 512, 128, 4, n).transpose(0, 1, 3, 2))
    if fmt == "e4m3":
        words = by_word.astype(ml_dtypes.float8_e4m3fn).view(np.uint8)
    else:
        c = by_word.astype(ml_dtypes.float4_e2m1fn).view(np.uint8) & 0xF
        words = (c[..., 0::2] | (c[..., 1::2] << 4)).reshape(k // 512, 128, 2 * n)
    return np.ascontiguousarray(words), np.ascontiguousarray(byte.astype(np.uint8).reshape(k // 512, 16, n))


def unpack_weight(words, scales, fmt):
    g, _, n = scales.shape
    words = np.ascontiguousarray(words).reshape(g, 128, n, -1)
    if fmt == "e4m3":
        vals = words.view(ml_dtypes.float8_e4m3fn).astype(np.float64)
    else:
        nib = np.empty((g, 128, n, 4), np.uint8)
        nib[..., 0::2] = words & 0xF
        nib[..., 1::2] = words >> 4
        vals = E2M1[nib]
    vals = vals * np.repeat(np.exp2(scales.astype(np.float64) - 127.0), 8, axis=1)[..., None]
    return vals.transpose(0, 1, 3, 2).reshape(g * 512, n)


def bf(x):
    return np.asarray(x, np.float32).astype(ml_dtypes.bfloat16)


def planes(Y):
    r, m = Y.shape
    b = f64(bf(Y)).reshape(r // 32, 32, m)
    amax = np.abs(b).max(1)
    byte = np.clip(np.where(amax > 0, np.frexp(amax)[1] - 1 + 127 - 7, 1), 1, 254)
    codes = (b * np.exp2(127.0 - byte)[:, None, :]).reshape(r, m).astype(np.float32).astype(ml_dtypes.float8_e4m3fn).view(np.uint8)
    words = codes.reshape(r // 512, 128, 4, m).transpose(0, 1, 3, 2)
    return np.ascontiguousarray(words), np.ascontiguousarray(byte.astype(np.uint8).reshape(r // 512, 16, m))


K, T, J, R, C, O, N, Z = 1024, 1024, 256, 512, 1024, 256, 512, 512


def setup_inputs():
    n = np.random.standard_normal
    idx = np.random.permutation(T)[:J]
    idx2 = np.random.permutation(C)[:J]
    idx3 = np.random.permutation(C)[:O]
    idx4 = np.random.permutation(Z)[:O]
    fk = mx_kscale(K)
    fr = mx_kscale(R)
    wp = pack_weight(n((K, R)) * 1 / np.sqrt(K) * fk[:, None] * fr, "e4m3")
    wbp = pack_weight(n((R, N)) * 1 / np.sqrt(R) / fr[:, None], "e2m1")
    return {
        "xf": (n((K, T))).astype(np.float32),
        "ow": (n((K, J)) * 0.7).astype(np.float32),
        "fk": (np.random.uniform(0.5, 2.0, (K, 1)) / fk[:, None]).astype(np.float32),
        "w_words": wp[0],
        "w_scales": wp[1],
        "oldh": (n((R, C)) * 0.7 * fr[:, None]).astype(np.float32),
        "wb_words": wbp[0],
        "wb_scales": wbp[1],
        "tz": (n((N, Z)) * 0.6).astype(np.float32),
        "rw": (np.random.uniform(0.5, 2.0, (1, O))).astype(np.float32),
        "offs": striped(idx),
        "offs2": striped(idx2),
        "offs3": striped(idx3),
        "offs4": striped(idx4),
    }


def reference(xf, ow, fk, w_words, w_scales, oldh, wb_words, wb_scales, tz, rw, offs, offs2, offs3, offs4):
    idx = unstriped(offs)
    idx2 = unstriped(offs2)
    idx3 = unstriped(offs3)
    idx4 = unstriped(offs4)
    wu = unpack_weight(w_words, w_scales, "e4m3")
    wbu = unpack_weight(wb_words, wb_scales, "e2m1")
    u = (f64(xf)[:, idx] - f64(ow)) * f64(fk)
    uq = mxq(u, 0, "e4m3")
    a = wu.T @ uq
    ha = np.maximum(a, 0.0)
    pw0 = np.zeros((R, C))
    pw0[:, idx2] = ha
    pg = pw0 + f64(oldh)
    hid = pg[:, idx3]
    hidq = mxq(hid, 0, "e5m2")
    p = wbu.T @ hidq
    y = np.maximum(p, f64(tz)[:, idx4]) * f64(rw)
    words, scales = planes(y)
    return y, words, scales

@@ -1,0 +1,251 @@
+from contextlib import ExitStack
+
+import concourse.mybir as mybir
+
+K, T, J, R, C, O, N, Z = 1024, 1024, 256, 512, 1024, 256, 512, 512
+FLOPS = 2 * K * R * J + 2 * R * N * O
+
+F32 = mybir.dt.float32
+BF16 = mybir.dt.bfloat16
+I32 = mybir.dt.int32
+U32 = mybir.dt.uint32
+U16 = mybir.dt.uint16
+U8 = mybir.dt.uint8
+E4M3 = mybir.dt.float8_e4m3fn_x4
+E5M2 = mybir.dt.float8_e5m2_x4
+E2M1 = mybir.dt.float4_e2m1fn_x4
+ALU = mybir.AluOpType
+ACT = mybir.ActivationFunctionType
+
+P = 128
+PACK = 4
+HALF = 128
+LIST_COLS = J // 16
+
+
+def tile_list_page_offsetpicks_floored_pl_kernel(
+    tc, xf, ow, fk, w_words, w_scales, oldh, wb_words, wb_scales, tz, rw, offs, offs2, offs3, offs4, out_0, out_1, out_2
+):
+    nc = tc.nc
+    with ExitStack() as ctx:
+        sb = ctx.enter_context(tc.tile_pool(name="sb", bufs=1))
+        ps = ctx.enter_context(tc.psum_pool(name="ps", bufs=1))
+
+        def tile(name, shape, dtype):
+            return sb.tile(shape, dtype, name=name, align_bytes=64)
+
+        def half_cols(h):
+            return slice(h * HALF, (h + 1) * HALF)
+
+        def half_list(lst, h):
+            return lst[:, h * LIST_COLS // 2 : (h + 1) * LIST_COLS // 2]
+
+        lists = [sb.tile([P, LIST_COLS], U16, name="list%d" % i) for i in range(4)]
+        w_raw = tile("w_raw", [P, 2, R], U32)
+        ws_raw = tile("ws_raw", [P, R], U8)
+        wb_raw = tile("wb_raw", [P, 2 * N], U8)
+        wbs_raw = tile("wbs_raw", [P, N], U8)
+        fk_sb = tile("fk_sb", [P, 2, PACK], F32)
+        ow_sb = [tile("ow%d" % a, [P, PACK, J], F32) for a in range(2)]
+        x_sb = [tile("x%d" % i, [P, T], F32) for i in range(2 * PACK)]
+        old_sb = [tile("old%d" % t, [P, C], F32) for t in range(PACK)]
+        tz_sb = [tile("tz%d" % t, [P, Z], F32) for t in range(PACK)]
+        rw_sb = tile("rw_sb", [P, O], F32)
+        placed = [tile("placed%d" % t, [P, C], F32) for t in range(PACK)]
+
+        nc.vector.memset(ws_raw[:].bitcast(I32), 0)
+        nc.vector.memset(wbs_raw[:].bitcast(I32), 0)
+        for t in range(PACK):
+            nc.vector.memset(placed[t][:], 0.0)
+
+        x_rows = xf.rearrange("(a p t) c -> a t p c", a=2, t=PACK)
+        ow_rows = ow.rearrange("(a p t) j -> a p t j", a=2, t=PACK)
+        old_rows = oldh.rearrange("(p t) c -> t p c", t=PACK)
+        tz_rows = tz.rearrange("(p t) z -> t p z", t=PACK)
+
+        def load_x(i):
+            nc.sync.dma_start(x_sb[i][:], x_rows[i // PACK, i % PACK])
+
+        nc.sync.dma_start(w_raw[:].bitcast(I32), w_words.rearrange("a p n t -> p a (n t)").bitcast(I32))
+        nc.sync.dma_start(lists[0][:], offs)
+        load_x(0)
+        nc.sync.dma_start(ow_sb[0][:], ow_rows[0])
+        nc.sync.dma_start(fk_sb[:], fk.rearrange("(a p t) o -> p a (t o)", a=2, t=PACK))
+        load_x(1)
+        for q in range(4):
+            nc.sync.dma_start(
+                ws_raw[32 * q : 32 * q + 8, :].bitcast(I32), w_scales[:, 4 * q : 4 * q + 4, :].bitcast(I32)
+            )
+        load_x(2)
+        load_x(3)
+        nc.sync.dma_start(wb_raw[:].bitcast(I32), wb_words[0].bitcast(I32))
+        nc.sync.dma_start(ow_sb[1][:], ow_rows[1])
+        for q in range(4):
+            nc.sync.dma_start(
+                wbs_raw[32 * q : 32 * q + 4, :].bitcast(I32), wb_scales[0, 4 * q : 4 * q + 4, :].bitcast(I32)
+            )
+        load_x(4)
+        load_x(5)
+        nc.sync.dma_start(lists[1][:], offs2)
+        load_x(6)
+        load_x(7)
+        nc.sync.dma_start(lists[3][:], offs4)
+        nc.sync.dma_start(tz_sb[0][:], tz_rows[0])
+        nc.sync.dma_start(lists[2][:], offs3)
+        for t in range(PACK):
+            nc.sync.dma_start(old_sb[t][:], old_rows[t])
+        for t in range(1, PACK):
+            nc.sync.dma_start(tz_sb[t][:], tz_rows[t])
+        nc.sync.dma_start(rw_sb[:], rw[0].partition_broadcast(P))
+
+        w_codes = tile("w_codes", [P, 2, R], U32)
+        w_sc = tile("w_sc", [P, R], U8)
+        wb_codes = tile("wb_codes", [P, 2 * N], U8)
+        wb_sc = tile("wb_sc", [P, N], U8)
+        for a in range(2):
+            nc.vector.tensor_copy(
+                w_codes[:, a, :].rearrange("p (t b i) -> p b t i", t=PACK, i=4),
+                w_raw[:, a, :].rearrange("p (b i t) -> p b t i", t=PACK, i=4),
+            )
+
+        def deal_scales(dst, src):
+            nc.vector.tensor_copy(
+                dst[:].rearrange("p (t b i) -> p b t i", t=PACK, i=16),
+                src[:].rearrange("p (b i t) -> p b t i", t=PACK, i=16),
+            )
+
+        def interleave(engine_copy, dst, src):
+            engine_copy(
+                dst.rearrange("p (b i t) -> p b t i", t=PACK, i=4),
+                src.rearrange("p t (b i) -> p b t i", i=4),
+            )
+
+        diff = [tile("diff%d" % a, [P, PACK, J], F32) for a in range(2)]
+        acc = [ps.tile([P, J], F32, name="acc%d" % t) for t in range(PACK)]
+
+        def centre(a, t, cols, lst):
+            nc.vector.tensor_tensor(
+                diff[a][:, t, cols], x_sb[PACK * a + t][:].indirect(lst), ow_sb[a][:, t, cols], ALU.subtract
+            )
+
+        def factor(a, t, cols, dst):
+            nc.scalar.activation(
+                dst[:].rearrange("p (j t) -> p j t", t=PACK)[:, :, t],
+                diff[a][:, t, cols],
+                ACT.Copy,
+                scale=fk_sb[:, a, t : t + 1],
+            )
+
+        def first_product(a, cols, u_bf, start, stop):
+            width = cols.stop - cols.start
+            codes = tile("u_codes%d_%d" % (a, cols.start), [P, width], U32)
+            scales = tile("u_sc%d_%d" % (a, cols.start), [P, width], U8)
+            nc.vector.quantize_mx(codes[:].bitcast(E4M3), scales[:], u_bf[:])
+            for t in range(PACK):
+                r_cols = slice(t * P, (t + 1) * P)
+                nc.tensor.matmul_mx(
+                    acc[t][:, cols],
+                    lhsT=w_codes[:, a, r_cols].bitcast(E4M3),
+                    lhsT_scale=w_sc[4 * a :, r_cols],
+                    rhs=codes[:].bitcast(E4M3),
+                    rhs_scale=scales[:],
+                    start=start,
+                    stop=stop,
+                )
+
+        whole = slice(0, J)
+        u0 = tile("u0", [P, PACK * J], BF16)
+        for t in range(PACK):
+            centre(0, t, whole, lists[0][:])
+            factor(0, t, whole, u0)
+            if t == 1:
+                deal_scales(w_sc, ws_raw)
+        first_product(0, whole, u0, True, False)
+        nc.vector.tensor_copy(
+            wb_codes[:].rearrange("p (t b i e) -> p b t i e", t=PACK, i=8, e=2),
+            wb_raw[:].rearrange("p (b i t e) -> p b t i e", t=PACK, i=8, e=2),
+        )
+        deal_scales(wb_sc, wbs_raw)
+
+        u1 = [tile("u1_%d" % h, [P, PACK * HALF], BF16) for h in range(2)]
+        for t in range(PACK):
+            if t < PACK - 1:
+                centre(1, t, whole, lists[0][:])
+            for h in range(2):
+                if t == PACK - 1:
+                    centre(1, t, half_cols(h), half_list(lists[0], h))
+                factor(1, t, half_cols(h), u1[h])
+        for h in range(2):
+            first_product(1, half_cols(h), u1[h], False, h == 1)
+
+        floor = tile("floor", [P, PACK, O], F32)
+
+        def pick_floor(t):
+            nc.scalar.activation(floor[:, t, :], tz_sb[t][:].indirect(lists[3][:]), ACT.Copy)
+
+        pick_floor(0)
+
+        ha = [tile("ha%d" % t, [P, J], F32) for t in range(PACK)]
+        page = [tile("page%d" % t, [P, C], F32) for t in range(PACK)]
+        hid = tile("hid", [P, PACK, O], BF16)
+        for t in range(PACK):
+            if t % 2 == 0:
+                nc.scalar.activation(ha[t][:], acc[t][:], ACT.Relu)
+            else:
+                nc.vector.tensor_scalar(ha[t][:], acc[t][:], 0.0, None, ALU.max)
+        for t in range(PACK):
+            if t == 1:
+                nc.vector.tensor_copy(placed[t][:].indirect(lists[1][:]), ha[t][:])
+            else:
+                nc.scalar.activation(placed[t][:].indirect(lists[1][:]), ha[t][:], ACT.Copy)
+        for t in range(PACK):
+            nc.vector.tensor_tensor(page[t][:], placed[t][:], old_sb[t][:], ALU.add)
+        for t in range(PACK - 1):
+            nc.scalar.activation(hid[:, t, :], page[t][:].indirect(lists[2][:]), ACT.Copy)
+        last = PACK - 1
+        nc.vector.tensor_copy(hid[:, last, half_cols(0)], page[last][:].indirect(half_list(lists[2], 0)))
+        nc.scalar.activation(hid[:, last, half_cols(1)], page[last][:].indirect(half_list(lists[2], 1)), ACT.Copy)
+        for t in range(1, PACK):
+            pick_floor(t)
+
+        hid_bf = [tile("hid_bf%d" % h, [P, PACK * HALF], BF16) for h in range(2)]
+        prod = [ps.tile([P, PACK, HALF], F32, name="prod%d" % h) for h in range(2)]
+        for h in range(2):
+            interleave(nc.vector.tensor_copy, hid_bf[h][:], hid[:, :, half_cols(h)])
+        for h in range(2):
+            codes = tile("h_codes%d" % h, [P, HALF], U32)
+            scales = tile("h_sc%d" % h, [P, HALF], U8)
+            nc.vector.quantize_mx(codes[:].bitcast(E5M2), scales[:], hid_bf[h][:])
+            for t in range(PACK):
+                nc.tensor.matmul_mx(
+                    prod[h][:, t, :],
+                    lhsT=wb_codes[:, 2 * t * P : 2 * (t + 1) * P].bitcast(E2M1),
+                    lhsT_scale=wb_sc[:, t * P : (t + 1) * P],
+                    rhs=codes[:].bitcast(E5M2),
+                    rhs_scale=scales[:],
+                    start=True,
+                    stop=True,
+                )
+
+        floored = [tile("floored%d" % h, [P, PACK, HALF], F32) for h in range(2)]
+        y = [tile("y%d" % h, [P, PACK, HALF], F32) for h in range(2)]
+        y_bf = [tile("y_bf%d" % h, [P, PACK * HALF], BF16) for h in range(2)]
+        y_codes = tile("y_codes", [P, O], U32)
+        y_sc = tile("y_sc", [P, O], U8)
+        y_rows = out_0.rearrange("(p t) o -> p t o", t=PACK)
+        word_rows = out_1[0].rearrange("p c t -> p (c t)").bitcast(I32)
+        for h in range(2):
+            nc.vector.tensor_tensor(floored[h][:], prod[h][:], floor[:, :, half_cols(h)], ALU.max)
+        for h in range(2):
+            nc.vector.tensor_tensor(
+                y[h][:], floored[h][:], rw_sb[:, half_cols(h)].unsqueeze(1).to_broadcast([P, PACK, HALF]), ALU.mult
+            )
+            nc.sync.dma_start(y_rows[:, :, half_cols(h)], y[h][:])
+        interleave(nc.scalar.copy, y_bf[0][:], y[0][:])
+        interleave(nc.vector.tensor_copy, y_bf[1][:], y[1][:])
+        for h in range(2):
+            nc.vector.quantize_mx(y_codes[:, half_cols(h)].bitcast(E4M3), y_sc[:, half_cols(h)], y_bf[h][:])
+        nc.sync.dma_start(word_rows, y_codes[:].bitcast(I32))
+        for q in range(4):
+            queue = nc.sync if q % 2 == 0 else nc.scalar
+            queue.dma_start(out_2[0, 4 * q : 4 * q + 4, :].bitcast(I32), y_sc[32 * q : 32 * q + 4, :].bitcast(I32))

@@ -41,7 +41,7 @@ def tile_list_page_offsetpicks_floored_pl_kernel(
             return lst[:, h * LIST_COLS // 2 : (h + 1) * LIST_COLS // 2]
 
         lists = [sb.tile([P, LIST_COLS], U16, name="list%d" % i) for i in range(4)]
-        w_raw = tile("w_raw", [P, 2, R], U32)
+        w_raw = [tile("w_raw%d" % a, [P, R], U32) for a in range(2)]
         ws_raw = tile("ws_raw", [P, R], U8)
         wb_raw = tile("wb_raw", [P, 2 * N], U8)
         wbs_raw = tile("wbs_raw", [P, N], U8)
@@ -49,7 +49,7 @@ def tile_list_page_offsetpicks_floored_pl_kernel(
         ow_sb = [tile("ow%d" % a, [P, PACK, J], F32) for a in range(2)]
         x_sb = [tile("x%d" % i, [P, T], F32) for i in range(2 * PACK)]
         old_sb = [tile("old%d" % t, [P, C], F32) for t in range(PACK)]
-        tz_sb = [tile("tz%d" % t, [P, Z], F32) for t in range(PACK)]
+        tz_sb = [sb.tile([P, Z], F32, name="tz%d" % t, tag="tz%d" % t, align_bytes=64) for t in range(PACK)]
         rw_sb = tile("rw_sb", [P, O], F32)
         placed = [tile("placed%d" % t, [P, C], F32) for t in range(PACK)]
 
@@ -66,7 +66,10 @@ def tile_list_page_offsetpicks_floored_pl_kernel(
         def load_x(i):
             nc.sync.dma_start(x_sb[i][:], x_rows[i // PACK, i % PACK])
 
-        nc.sync.dma_start(w_raw[:].bitcast(I32), w_words.rearrange("a p n t -> p a (n t)").bitcast(I32))
+        def load_w(a):
+            nc.sync.dma_start(w_raw[a][:].bitcast(I32), w_words[a].rearrange("p n t -> p (n t)").bitcast(I32))
+
+        load_w(0)
         nc.sync.dma_start(lists[0][:], offs)
         load_x(0)
         nc.sync.dma_start(ow_sb[0][:], ow_rows[0])
@@ -89,24 +92,29 @@ def tile_list_page_offsetpicks_floored_pl_kernel(
         nc.sync.dma_start(lists[1][:], offs2)
         load_x(6)
         load_x(7)
+        load_w(1)
         nc.sync.dma_start(lists[3][:], offs4)
-        nc.sync.dma_start(tz_sb[0][:], tz_rows[0])
+        for t in range(2):
+            nc.sync.dma_start(tz_sb[t][:], tz_rows[t])
         nc.sync.dma_start(lists[2][:], offs3)
         for t in range(PACK):
             nc.sync.dma_start(old_sb[t][:], old_rows[t])
-        for t in range(1, PACK):
+        for t in range(2, PACK):
             nc.sync.dma_start(tz_sb[t][:], tz_rows[t])
         nc.sync.dma_start(rw_sb[:], rw[0].partition_broadcast(P))
 
-        w_codes = tile("w_codes", [P, 2, R], U32)
+        w_codes = [tile("w_codes%d" % a, [P, R], U32) for a in range(2)]
         w_sc = tile("w_sc", [P, R], U8)
         wb_codes = tile("wb_codes", [P, 2 * N], U8)
         wb_sc = tile("wb_sc", [P, N], U8)
-        for a in range(2):
+
+        def deal_words(a):
             nc.vector.tensor_copy(
-                w_codes[:, a, :].rearrange("p (t b i) -> p b t i", t=PACK, i=4),
-                w_raw[:, a, :].rearrange("p (b i t) -> p b t i", t=PACK, i=4),
+                w_codes[a][:].rearrange("p (t b i) -> p b t i", t=PACK, i=4),
+                w_raw[a][:].rearrange("p (b i t) -> p b t i", t=PACK, i=4),
             )
+
+        deal_words(0)
 
         def deal_scales(dst, src):
             nc.vector.tensor_copy(
@@ -145,7 +153,7 @@ def tile_list_page_offsetpicks_floored_pl_kernel(
                 r_cols = slice(t * P, (t + 1) * P)
                 nc.tensor.matmul_mx(
                     acc[t][:, cols],
-                    lhsT=w_codes[:, a, r_cols].bitcast(E4M3),
+                    lhsT=w_codes[a][:, r_cols].bitcast(E4M3),
                     lhsT_scale=w_sc[4 * a :, r_cols],
                     rhs=codes[:].bitcast(E4M3),
                     rhs_scale=scales[:],
@@ -175,41 +183,44 @@ def tile_list_page_offsetpicks_floored_pl_kernel(
                 if t == PACK - 1:
                     centre(1, t, half_cols(h), half_list(lists[0], h))
                 factor(1, t, half_cols(h), u1[h])
+        deal_words(1)
         for h in range(2):
             first_product(1, half_cols(h), u1[h], False, h == 1)
 
-        floor = tile("floor", [P, PACK, O], F32)
+        floor_early = tile("floor_early", [P, 2, O], F32)
+        nc.scalar.activation(floor_early[:, 0, :], tz_sb[0][:].indirect(lists[3][:]), ACT.Copy)
+        nc.vector.tensor_copy(floor_early[:, 1, :], tz_sb[1][:].indirect(lists[3][:]))
 
-        def pick_floor(t):
-            nc.scalar.activation(floor[:, t, :], tz_sb[t][:].indirect(lists[3][:]), ACT.Copy)
-
-        pick_floor(0)
-
-        ha = [tile("ha%d" % t, [P, J], F32) for t in range(PACK)]
-        page = [tile("page%d" % t, [P, C], F32) for t in range(PACK)]
+        ha_by = [sb.tile([P, 2, J], F32, name="ha%d" % e, tag="tz%d" % e, align_bytes=64) for e in range(2)]
+        ha = [ha_by[t % 2][:, t // 2, :] for t in range(PACK)]
+        page = [sb.tile([P, C], F32, name="page%d" % t, tag="page%d" % t, align_bytes=64) for t in range(PACK)]
         hid = tile("hid", [P, PACK, O], BF16)
         for t in range(PACK):
             if t % 2 == 0:
-                nc.scalar.activation(ha[t][:], acc[t][:], ACT.Relu)
+                nc.scalar.activation(ha[t], acc[t][:], ACT.Relu)
             else:
-                nc.vector.tensor_scalar(ha[t][:], acc[t][:], 0.0, None, ALU.max)
+                nc.vector.tensor_scalar(ha[t], acc[t][:], 0.0, None, ALU.max)
         for t in range(PACK):
             if t == 1:
-                nc.vector.tensor_copy(placed[t][:].indirect(lists[1][:]), ha[t][:])
+                nc.vector.tensor_copy(placed[t][:].indirect(lists[1][:]), ha[t])
             else:
-                nc.scalar.activation(placed[t][:].indirect(lists[1][:]), ha[t][:], ACT.Copy)
+                nc.scalar.activation(placed[t][:].indirect(lists[1][:]), ha[t], ACT.Copy)
         for t in range(PACK):
             nc.vector.tensor_tensor(page[t][:], placed[t][:], old_sb[t][:], ALU.add)
-        for t in range(PACK - 1):
-            nc.scalar.activation(hid[:, t, :], page[t][:].indirect(lists[2][:]), ACT.Copy)
         last = PACK - 1
+        for t in range(PACK - 2):
+            nc.scalar.activation(hid[:, t, :], page[t][:].indirect(lists[2][:]), ACT.Copy)
+        for h in range(2):
+            nc.scalar.activation(hid[:, 2, half_cols(h)], page[2][:].indirect(half_list(lists[2], h)), ACT.Copy)
         nc.vector.tensor_copy(hid[:, last, half_cols(0)], page[last][:].indirect(half_list(lists[2], 0)))
         nc.scalar.activation(hid[:, last, half_cols(1)], page[last][:].indirect(half_list(lists[2], 1)), ACT.Copy)
-        for t in range(1, PACK):
-            pick_floor(t)
+        floor_rest = sb.tile([P, 2, 2, HALF], F32, name="floor_rest", tag="page3", align_bytes=64)
+        for h in range(2):
+            for t in range(2, PACK):
+                nc.scalar.activation(floor_rest[:, h, t - 2, :], tz_sb[t][:].indirect(half_list(lists[3], h)), ACT.Copy)
 
         hid_bf = [tile("hid_bf%d" % h, [P, PACK * HALF], BF16) for h in range(2)]
-        prod = [ps.tile([P, PACK, HALF], F32, name="prod%d" % h) for h in range(2)]
+        prod = [[ps.tile([P, 2, HALF], F32, name="prod%d_%d" % (h, u)) for u in range(2)] for h in range(2)]
         for h in range(2):
             interleave(nc.vector.tensor_copy, hid_bf[h][:], hid[:, :, half_cols(h)])
         for h in range(2):
@@ -218,7 +229,7 @@ def tile_list_page_offsetpicks_floored_pl_kernel(
             nc.vector.quantize_mx(codes[:].bitcast(E5M2), scales[:], hid_bf[h][:])
             for t in range(PACK):
                 nc.tensor.matmul_mx(
-                    prod[h][:, t, :],
+                    prod[h][t // 2][:, t % 2, :],
                     lhsT=wb_codes[:, 2 * t * P : 2 * (t + 1) * P].bitcast(E2M1),
                     lhsT_scale=wb_sc[:, t * P : (t + 1) * P],
                     rhs=codes[:].bitcast(E5M2),
@@ -235,7 +246,8 @@ def tile_list_page_offsetpicks_floored_pl_kernel(
         y_rows = out_0.rearrange("(p t) o -> p t o", t=PACK)
         word_rows = out_1[0].rearrange("p c t -> p (c t)").bitcast(I32)
         for h in range(2):
-            nc.vector.tensor_tensor(floored[h][:], prod[h][:], floor[:, :, half_cols(h)], ALU.max)
+            nc.vector.tensor_tensor(floored[h][:, :2, :], prod[h][0][:], floor_early[:, :, half_cols(h)], ALU.max)
+            nc.vector.tensor_tensor(floored[h][:, 2:, :], prod[h][1][:], floor_rest[:, h, :, :], ALU.max)
         for h in range(2):
             nc.vector.tensor_tensor(
                 y[h][:], floored[h][:], rw_sb[:, half_cols(h)].unsqueeze(1).to_broadcast([P, PACK, HALF]), ALU.mult

@@ -69,33 +69,34 @@ def tile_list_page_offsetpicks_floored_pl_kernel(
         def load_w(a):
             nc.sync.dma_start(w_raw[a][:].bitcast(I32), w_words[a].rearrange("p n t -> p (n t)").bitcast(I32))
 
-        load_w(0)
-        nc.sync.dma_start(lists[0][:], offs)
-        load_x(0)
-        nc.sync.dma_start(ow_sb[0][:], ow_rows[0])
-        nc.sync.dma_start(fk_sb[:], fk.rearrange("(a p t) o -> p a (t o)", a=2, t=PACK))
-        load_x(1)
-        for q in range(4):
+        def load_w_scales(q):
             nc.sync.dma_start(
                 ws_raw[32 * q : 32 * q + 8, :].bitcast(I32), w_scales[:, 4 * q : 4 * q + 4, :].bitcast(I32)
             )
-        load_x(2)
-        load_x(3)
+
         nc.sync.dma_start(wb_raw[:].bitcast(I32), wb_words[0].bitcast(I32))
-        nc.sync.dma_start(ow_sb[1][:], ow_rows[1])
+        load_w(0)
+        load_x(0)
+        nc.sync.dma_start(ow_sb[0][:], ow_rows[0])
+        nc.sync.dma_start(lists[0][:], offs)
+        nc.sync.dma_start(fk_sb[:], fk.rearrange("(a p t) o -> p a (t o)", a=2, t=PACK))
+        for q in range(3):
+            load_w_scales(q)
+        for i in range(1, PACK):
+            load_x(i)
+        load_w_scales(3)
         for q in range(4):
             nc.sync.dma_start(
                 wbs_raw[32 * q : 32 * q + 4, :].bitcast(I32), wb_scales[0, 4 * q : 4 * q + 4, :].bitcast(I32)
             )
-        load_x(4)
-        load_x(5)
-        nc.sync.dma_start(lists[1][:], offs2)
-        load_x(6)
-        load_x(7)
+        nc.sync.dma_start(ow_sb[1][:], ow_rows[1])
+        for i in range(PACK, 2 * PACK):
+            load_x(i)
         load_w(1)
         nc.sync.dma_start(lists[3][:], offs4)
         for t in range(2):
             nc.sync.dma_start(tz_sb[t][:], tz_rows[t])
+        nc.sync.dma_start(lists[1][:], offs2)
         nc.sync.dma_start(lists[2][:], offs3)
         for t in range(PACK):
             nc.sync.dma_start(old_sb[t][:], old_rows[t])
@@ -114,6 +115,10 @@ def tile_list_page_offsetpicks_floored_pl_kernel(
                 w_raw[a][:].rearrange("p (b i t) -> p b t i", t=PACK, i=4),
             )
 
+        nc.vector.tensor_copy(
+            wb_codes[:].rearrange("p (t b i e) -> p b t i e", t=PACK, i=8, e=2),
+            wb_raw[:].rearrange("p (b i t e) -> p b t i e", t=PACK, i=8, e=2),
+        )
         deal_words(0)
 
         def deal_scales(dst, src):
@@ -166,14 +171,9 @@ def tile_list_page_offsetpicks_floored_pl_kernel(
         for t in range(PACK):
             centre(0, t, whole, lists[0][:])
             factor(0, t, whole, u0)
-            if t == 1:
-                deal_scales(w_sc, ws_raw)
-        first_product(0, whole, u0, True, False)
-        nc.vector.tensor_copy(
-            wb_codes[:].rearrange("p (t b i e) -> p b t i e", t=PACK, i=8, e=2),
-            wb_raw[:].rearrange("p (b i t e) -> p b t i e", t=PACK, i=8, e=2),
-        )
+        deal_scales(w_sc, ws_raw)
         deal_scales(wb_sc, wbs_raw)
+        first_product(0, whole, u0, True, False)
 
         u1 = [tile("u1_%d" % h, [P, PACK * HALF], BF16) for h in range(2)]
         for t in range(PACK):

from contextlib import ExitStack

import concourse.mybir as mybir

K, T, J, R, C, O, N, Z = 1024, 1024, 256, 512, 1024, 256, 512, 512
FLOPS = 2 * K * R * J + 2 * R * N * O

F32 = mybir.dt.float32
BF16 = mybir.dt.bfloat16
I32 = mybir.dt.int32
U32 = mybir.dt.uint32
U16 = mybir.dt.uint16
U8 = mybir.dt.uint8
E4M3 = mybir.dt.float8_e4m3fn_x4
E5M2 = mybir.dt.float8_e5m2_x4
E2M1 = mybir.dt.float4_e2m1fn_x4
ALU = mybir.AluOpType
ACT = mybir.ActivationFunctionType

P = 128
PACK = 4
HALF = 128
LIST_COLS = J // 16


def tile_list_page_offsetpicks_floored_pl_kernel(
    tc, xf, ow, fk, w_words, w_scales, oldh, wb_words, wb_scales, tz, rw, offs, offs2, offs3, offs4, out_0, out_1, out_2
):
    nc = tc.nc
    with ExitStack() as ctx:
        sb = ctx.enter_context(tc.tile_pool(name="sb", bufs=1))
        ps = ctx.enter_context(tc.psum_pool(name="ps", bufs=1))

        def tile(name, shape, dtype):
            return sb.tile(shape, dtype, name=name, align_bytes=64)

        def half_cols(h):
            return slice(h * HALF, (h + 1) * HALF)

        def half_list(lst, h):
            return lst[:, h * LIST_COLS // 2 : (h + 1) * LIST_COLS // 2]

        lists = [sb.tile([P, LIST_COLS], U16, name="list%d" % i) for i in range(4)]
        w_raw = [tile("w_raw%d" % a, [P, R], U32) for a in range(2)]
        ws_raw = tile("ws_raw", [P, R], U8)
        wb_raw = tile("wb_raw", [P, 2 * N], U8)
        wbs_raw = tile("wbs_raw", [P, N], U8)
        fk_sb = tile("fk_sb", [P, 2, PACK], F32)
        ow_sb = [tile("ow%d" % a, [P, PACK, J], F32) for a in range(2)]
        x_sb = [tile("x%d" % i, [P, T], F32) for i in range(2 * PACK)]
        old_sb = [tile("old%d" % t, [P, C], F32) for t in range(PACK)]
        tz_sb = [sb.tile([P, Z], F32, name="tz%d" % t, tag="tz%d" % t, align_bytes=64) for t in range(PACK)]
        rw_sb = tile("rw_sb", [P, O], F32)
        placed = [tile("placed%d" % t, [P, C], F32) for t in range(PACK)]

        nc.vector.memset(ws_raw[:].bitcast(I32), 0)
        nc.vector.memset(wbs_raw[:].bitcast(I32), 0)
        for t in range(PACK):
            nc.vector.memset(placed[t][:], 0.0)

        x_rows = xf.rearrange("(a p t) c -> a t p c", a=2, t=PACK)
        ow_rows = ow.rearrange("(a p t) j -> a p t j", a=2, t=PACK)
        old_rows = oldh.rearrange("(p t) c -> t p c", t=PACK)
        tz_rows = tz.rearrange("(p t) z -> t p z", t=PACK)

        def load_x(i):
            nc.sync.dma_start(x_sb[i][:], x_rows[i // PACK, i % PACK])

        def load_w(a):
            nc.sync.dma_start(w_raw[a][:].bitcast(I32), w_words[a].rearrange("p n t -> p (n t)").bitcast(I32))

        def load_w_scales(q):
            nc.sync.dma_start(
                ws_raw[32 * q : 32 * q + 8, :].bitcast(I32), w_scales[:, 4 * q : 4 * q + 4, :].bitcast(I32)
            )

        nc.sync.dma_start(wb_raw[:].bitcast(I32), wb_words[0].bitcast(I32))
        load_w(0)
        load_x(0)
        nc.sync.dma_start(ow_sb[0][:], ow_rows[0])
        nc.sync.dma_start(lists[0][:], offs)
        nc.sync.dma_start(fk_sb[:], fk.rearrange("(a p t) o -> p a (t o)", a=2, t=PACK))
        for q in range(3):
            load_w_scales(q)
        for i in range(1, PACK):
            load_x(i)
        load_w_scales(3)
        for q in range(4):
            nc.sync.dma_start(
                wbs_raw[32 * q : 32 * q + 4, :].bitcast(I32), wb_scales[0, 4 * q : 4 * q + 4, :].bitcast(I32)
            )
        nc.sync.dma_start(ow_sb[1][:], ow_rows[1])
        for i in range(PACK, 2 * PACK):
            load_x(i)
        load_w(1)
        nc.sync.dma_start(lists[3][:], offs4)
        for t in range(2):
            nc.sync.dma_start(tz_sb[t][:], tz_rows[t])
        nc.sync.dma_start(lists[1][:], offs2)
        nc.sync.dma_start(lists[2][:], offs3)
        for t in range(PACK):
            nc.sync.dma_start(old_sb[t][:], old_rows[t])
        for t in range(2, PACK):
            nc.sync.dma_start(tz_sb[t][:], tz_rows[t])
        nc.sync.dma_start(rw_sb[:], rw[0].partition_broadcast(P))

        w_codes = [tile("w_codes%d" % a, [P, R], U32) for a in range(2)]
        w_sc = tile("w_sc", [P, R], U8)
        wb_codes = tile("wb_codes", [P, 2 * N], U8)
        wb_sc = tile("wb_sc", [P, N], U8)

        def deal_words(a):
            nc.vector.tensor_copy(
                w_codes[a][:].rearrange("p (t b i) -> p b t i", t=PACK, i=4),
                w_raw[a][:].rearrange("p (b i t) -> p b t i", t=PACK, i=4),
            )

        nc.vector.tensor_copy(
            wb_codes[:].rearrange("p (t b i e) -> p b t i e", t=PACK, i=8, e=2),
            wb_raw[:].rearrange("p (b i t e) -> p b t i e", t=PACK, i=8, e=2),
        )
        deal_words(0)

        def deal_scales(dst, src):
            nc.vector.tensor_copy(
                dst[:].rearrange("p (t b i) -> p b t i", t=PACK, i=16),
                src[:].rearrange("p (b i t) -> p b t i", t=PACK, i=16),
            )

        def interleave(engine_copy, dst, src):
            engine_copy(
                dst.rearrange("p (b i t) -> p b t i", t=PACK, i=4),
                src.rearrange("p t (b i) -> p b t i", i=4),
            )

        diff = [tile("diff%d" % a, [P, PACK, J], F32) for a in range(2)]
        acc = [ps.tile([P, J], F32, name="acc%d" % t) for t in range(PACK)]

        def centre(a, t, cols, lst):
            nc.vector.tensor_tensor(
                diff[a][:, t, cols], x_sb[PACK * a + t][:].indirect(lst), ow_sb[a][:, t, cols], ALU.subtract
            )

        def factor(a, t, cols, dst):
            nc.scalar.activation(
                dst[:].rearrange("p (j t) -> p j t", t=PACK)[:, :, t],
                diff[a][:, t, cols],
                ACT.Copy,
                scale=fk_sb[:, a, t : t + 1],
            )

        def first_product(a, cols, u_bf, start, stop):
            width = cols.stop - cols.start
            codes = tile("u_codes%d_%d" % (a, cols.start), [P, width], U32)
            scales = tile("u_sc%d_%d" % (a, cols.start), [P, width], U8)
            nc.vector.quantize_mx(codes[:].bitcast(E4M3), scales[:], u_bf[:])
            for t in range(PACK):
                r_cols = slice(t * P, (t + 1) * P)
                nc.tensor.matmul_mx(
                    acc[t][:, cols],
                    lhsT=w_codes[a][:, r_cols].bitcast(E4M3),
                    lhsT_scale=w_sc[4 * a :, r_cols],
                    rhs=codes[:].bitcast(E4M3),
                    rhs_scale=scales[:],
                    start=start,
                    stop=stop,
                )

        whole = slice(0, J)
        u0 = tile("u0", [P, PACK * J], BF16)
        for t in range(PACK):
            centre(0, t, whole, lists[0][:])
            factor(0, t, whole, u0)
        deal_scales(w_sc, ws_raw)
        deal_scales(wb_sc, wbs_raw)
        first_product(0, whole, u0, True, False)

        u1 = [tile("u1_%d" % h, [P, PACK * HALF], BF16) for h in range(2)]
        for t in range(PACK):
            if t < PACK - 1:
                centre(1, t, whole, lists[0][:])
            for h in range(2):
                if t == PACK - 1:
                    centre(1, t, half_cols(h), half_list(lists[0], h))
                factor(1, t, half_cols(h), u1[h])
        deal_words(1)
        for h in range(2):
            first_product(1, half_cols(h), u1[h], False, h == 1)

        floor_early = tile("floor_early", [P, 2, O], F32)
        nc.scalar.activation(floor_early[:, 0, :], tz_sb[0][:].indirect(lists[3][:]), ACT.Copy)
        nc.vector.tensor_copy(floor_early[:, 1, :], tz_sb[1][:].indirect(lists[3][:]))

        ha_by = [sb.tile([P, 2, J], F32, name="ha%d" % e, tag="tz%d" % e, align_bytes=64) for e in range(2)]
        ha = [ha_by[t % 2][:, t // 2, :] for t in range(PACK)]
        page = [sb.tile([P, C], F32, name="page%d" % t, tag="page%d" % t, align_bytes=64) for t in range(PACK)]
        hid = tile("hid", [P, PACK, O], BF16)
        for t in range(PACK):
            if t % 2 == 0:
                nc.scalar.activation(ha[t], acc[t][:], ACT.Relu)
            else:
                nc.vector.tensor_scalar(ha[t], acc[t][:], 0.0, None, ALU.max)
        for t in range(PACK):
            if t == 1:
                nc.vector.tensor_copy(placed[t][:].indirect(lists[1][:]), ha[t])
            else:
                nc.scalar.activation(placed[t][:].indirect(lists[1][:]), ha[t], ACT.Copy)
        for t in range(PACK):
            nc.vector.tensor_tensor(page[t][:], placed[t][:], old_sb[t][:], ALU.add)
        last = PACK - 1
        for t in range(PACK - 2):
            nc.scalar.activation(hid[:, t, :], page[t][:].indirect(lists[2][:]), ACT.Copy)
        for h in range(2):
            nc.scalar.activation(hid[:, 2, half_cols(h)], page[2][:].indirect(half_list(lists[2], h)), ACT.Copy)
        nc.vector.tensor_copy(hid[:, last, half_cols(0)], page[last][:].indirect(half_list(lists[2], 0)))
        nc.scalar.activation(hid[:, last, half_cols(1)], page[last][:].indirect(half_list(lists[2], 1)), ACT.Copy)
        floor_rest = sb.tile([P, 2, 2, HALF], F32, name="floor_rest", tag="page3", align_bytes=64)
        for h in range(2):
            for t in range(2, PACK):
                nc.scalar.activation(floor_rest[:, h, t - 2, :], tz_sb[t][:].indirect(half_list(lists[3], h)), ACT.Copy)

        hid_bf = [tile("hid_bf%d" % h, [P, PACK * HALF], BF16) for h in range(2)]
        prod = [[ps.tile([P, 2, HALF], F32, name="prod%d_%d" % (h, u)) for u in range(2)] for h in range(2)]
        for h in range(2):
            interleave(nc.vector.tensor_copy, hid_bf[h][:], hid[:, :, half_cols(h)])
        for h in range(2):
            codes = tile("h_codes%d" % h, [P, HALF], U32)
            scales = tile("h_sc%d" % h, [P, HALF], U8)
            nc.vector.quantize_mx(codes[:].bitcast(E5M2), scales[:], hid_bf[h][:])
            for t in range(PACK):
                nc.tensor.matmul_mx(
                    prod[h][t // 2][:, t % 2, :],
                    lhsT=wb_codes[:, 2 * t * P : 2 * (t + 1) * P].bitcast(E2M1),
                    lhsT_scale=wb_sc[:, t * P : (t + 1) * P],
                    rhs=codes[:].bitcast(E5M2),
                    rhs_scale=scales[:],
                    start=True,
                    stop=True,
                )

        floored = [tile("floored%d" % h, [P, PACK, HALF], F32) for h in range(2)]
        y = [tile("y%d" % h, [P, PACK, HALF], F32) for h in range(2)]
        y_bf = [tile("y_bf%d" % h, [P, PACK * HALF], BF16) for h in range(2)]
        y_codes = tile("y_codes", [P, O], U32)
        y_sc = tile("y_sc", [P, O], U8)
        y_rows = out_0.rearrange("(p t) o -> p t o", t=PACK)
        word_rows = out_1[0].rearrange("p c t -> p (c t)").bitcast(I32)
        for h in range(2):
            nc.vector.tensor_tensor(floored[h][:, :2, :], prod[h][0][:], floor_early[:, :, half_cols(h)], ALU.max)
            nc.vector.tensor_tensor(floored[h][:, 2:, :], prod[h][1][:], floor_rest[:, h, :, :], ALU.max)
        for h in range(2):
            nc.vector.tensor_tensor(
                y[h][:], floored[h][:], rw_sb[:, half_cols(h)].unsqueeze(1).to_broadcast([P, PACK, HALF]), ALU.mult
            )
            nc.sync.dma_start(y_rows[:, :, half_cols(h)], y[h][:])
        interleave(nc.scalar.copy, y_bf[0][:], y[0][:])
        interleave(nc.vector.tensor_copy, y_bf[1][:], y[1][:])
        for h in range(2):
            nc.vector.quantize_mx(y_codes[:, half_cols(h)].bitcast(E4M3), y_sc[:, half_cols(h)], y_bf[h][:])
        nc.sync.dma_start(word_rows, y_codes[:].bitcast(I32))
        for q in range(4):
            queue = nc.sync if q % 2 == 0 else nc.scalar
            queue.dma_start(out_2[0, 4 * q : 4 * q + 4, :].bitcast(I32), y_sc[32 * q : 32 * q + 4, :].bitcast(I32))
